import numpy as np
import ml_dtypes


def mxq(x, axis, fmt="e4m3"):
    dtype, down = {"e4m3": (ml_dtypes.float8_e4m3fn, 7), "e5m2": (ml_dtypes.float8_e5m2, 14)}[fmt]
    v = np.moveaxis(np.asarray(x, np.float32).astype(ml_dtypes.bfloat16).astype(np.float64), axis, -1)
    blocks = v.reshape(v.shape[:-1] + (-1, 32))
    amax = np.abs(blocks).max(-1, keepdims=True)
    byte = np.maximum(np.where(amax > 0, np.frexp(amax)[1] - 1 + 127, 0) - down, 1)
    scale = np.exp2(byte - 127.0)
    codes = (blocks / scale).astype(np.float32).astype(dtype).astype(np.float64)
    return np.moveaxis((codes * scale).reshape(v.shape), -1, axis)


WIDE = False


def mx_kscale(k):
    if not WIDE:
        return np.ones(k)
    levels = np.array([10, -10, 5, -5, 0])
    if k % 512:
        return np.exp2(np.random.permutation(np.resize(levels, k // 32))).repeat(32)
    a = np.empty((k // 512, 16))
    for p in range(k // 512):
        a[p, :8] = np.random.permutation(np.resize(levels, 8))
        for g in range(8):
            far = levels[np.abs(levels - a[p, g]) >= 10]
            a[p, g + 8] = far[np.random.randint(len(far))]
    return np.exp2(a.ravel()).repeat(32)


def f64(x):
    return np.asarray(x).astype(np.float64)


def striped(idx):
    return np.tile(np.asarray(idx).reshape(-1, 16).T, (8, 1)).astype(np.uint16)


def unstriped(offs):
    return offs[:16].T.reshape(-1).astype(np.int64)


E2M1 = np.array([0.0, 0.5, 1.0, 1.5, 2.0, 3.0, 4.0, 6.0, -0.0, -0.5, -1.0, -1.5, -2.0, -3.0, -4.0, -6.0])


def pack_weight(w, fmt):
    k, n = w.shape
    w = f64(np.asarray(w, np.float32).astype(ml_dtypes.bfloat16)).reshape(k // 32, 32, n)
    amax = np.abs(w).max(1)
    if fmt == "e4m3":
        byte = np.frexp(amax)[1] - 1 + 127 - 7
    else:
        mant, ex = np.frexp(amax / 6.0)
        byte = np.where(mant > 0.5, ex, ex - 1) + 127
    byte = np.clip(np.where(amax > 0, byte, 1), 1, 254)
    scaled = (w * np.exp2(127.0 - byte)[:, None, :]).reshape(k, n).astype(np.float32)
    by_word = np.ascontiguousarray(scaled.reshape(k // 512, 128, 4, n).transpose(0, 1, 3, 2))
    if fmt == "e4m3":
        words = by_word.astype(ml_dtypes.float8_e4m3fn).view(np.uint8)
    else:
        c = by_word.astype(ml_dtypes.float4_e2m1fn).view(np.uint8) & 0xF
        words = (c[..., 0::2] | (c[..., 1::2] << 4)).reshape(k // 512, 128, 2 * n)
    return np.ascontiguousarray(words), np.ascontiguousarray(byte.astype(np.uint8).reshape(k // 512, 16, n))


def unpack_weight(words, scales, fmt):
    g, _, n = scales.shape
    words = np.ascontiguousarray(words).reshape(g, 128, n, -1)
    if fmt == "e4m3":
        vals = words.view(ml_dtypes.float8_e4m3fn).astype(np.float64)
    else:
        nib = np.empty((g, 128, n, 4), np.uint8)
        nib[..., 0::2] = words & 0xF
        nib[..., 1::2] = words >> 4
        vals = E2M1[nib]
    vals = vals * np.repeat(np.exp2(scales.astype(np.float64) - 127.0), 8, axis=1)[..., None]
    return vals.transpose(0, 1, 3, 2).reshape(g * 512, n)


def sigmoid(v):
    return 1.0 / (1.0 + np.exp(-v))


def bf(x):
    return np.asarray(x, np.float32).astype(ml_dtypes.bfloat16)


def planes(Y):
    r, m = Y.shape
    b = f64(bf(Y)).reshape(r // 32, 32, m)
    amax = np.abs(b).max(1)
    byte = np.clip(np.where(amax > 0, np.frexp(amax)[1] - 1 + 127 - 7, 1), 1, 254)
    codes = (b * np.exp2(127.0 - byte)[:, None, :]).reshape(r, m).astype(np.float32).astype(ml_dtypes.float8_e4m3fn).view(np.uint8)
    words = codes.reshape(r // 512, 128, 4, m).transpose(0, 1, 3, 2)
    return np.ascontiguousarray(words), np.ascontiguousarray(byte.astype(np.uint8).reshape(r // 512, 16, m))


D, E, T, I, Q = 512, 512, 2048, 512, 256


def setup_inputs():
    n = np.random.standard_normal
    idx = np.random.permutation(T)[:I]
    fd = mx_kscale(D)
    fi = mx_kscale(I)
    ti = np.ones(T)
    ti[idx] = fi
    keysp = pack_weight(n((D, T)) / fd[:, None], "e2m1")
    return {
        "query": (n((D, Q)) * 0.8 / np.sqrt(D) * fd[:, None]).astype(np.float32),
        "keys_words": keysp[0],
        "keys_scales": keysp[1],
        "share": (np.random.uniform(0.2, 0.8, (Q, 1))).astype(np.float32),
        "os": (np.random.uniform(4.0, 16.0, (1, I)) * fi).astype(np.float32),
        "vals": (n((E, T)) / ti).astype(np.float32),
        "offs": striped(idx),
    }


def reference(query, keys_words, keys_scales, share, os, vals, offs):
    idx = unstriped(offs)
    keysu = unpack_weight(keys_words, keys_scales, "e2m1")
    queryq = mxq(f64(query), 0, "e4m3")
    keysidxg = keysu[:, idx]
    a = queryq.T @ keysidxg
    e0 = np.exp(a)
    s0 = sigmoid(a)
    p = e0 * f64(share) + s0 * (1.0 - f64(share)) * 3.0
    z = np.sum(p, axis=1, keepdims=True)
    w = p / z
    wo1 = w * f64(os)
    wt1 = wo1.T
    vt1 = f64(vals)[:, idx].T
    vt1q = mxq(vt1, 0, "e4m3")
    wt1q = mxq(wt1, 0, "e4m3")
    o = vt1q.T @ wt1q
    words, scales = planes(o)
    return o, words, scales

@@ -1,0 +1,206 @@
+from contextlib import ExitStack
+
+import concourse.mybir as mybir
+from concourse.masks import make_identity
+
+D, E, T, SLOTS, Q = 512, 512, 2048, 512, 256
+FLOPS = 2 * Q * SLOTS * D + 2 * E * SLOTS * Q
+
+F32 = mybir.dt.float32
+BF16 = mybir.dt.bfloat16
+I32 = mybir.dt.int32
+U32 = mybir.dt.uint32
+U16 = mybir.dt.uint16
+U8 = mybir.dt.uint8
+FP8X4 = mybir.dt.float8_e4m3fn_x4
+FP4X4 = mybir.dt.float4_e2m1fn_x4
+ALU = mybir.AluOpType
+ACT = mybir.ActivationFunctionType
+AXIS = mybir.AxisListType
+
+P = 128
+PACK = 4
+HALVES = Q // P
+QUADRANT = 32
+TINY = 1e-30
+
+
+def tile_attend_mixedparts_pl_kernel(tc, query, keys_words, keys_scales, share, slot_factor, vals, offs, out_0, out_1, out_2):
+    nc = tc.nc
+    with ExitStack() as ctx:
+        sb = ctx.enter_context(tc.tile_pool(name="sb", bufs=1))
+        ps = ctx.enter_context(tc.psum_pool(name="ps", bufs=1))
+
+        offsets = sb.tile([P, SLOTS // 16], U16, name="offsets")
+        nc.sync.dma_start(offsets[:], offs)
+
+        share_col = sb.tile([P, HALVES], F32, name="share_col")
+        with nc.allow_non_contiguous_dma(reason="one share for each partition and half"):
+            nc.sync.dma_start(share_col[:], share.rearrange("(h p) o -> p (h o)", p=P))
+        key_words = sb.tile([P, T], U16, name="key_words", tag="slot_2", align_bytes=64)
+        nc.sync.dma_start(key_words[:].bitcast(I32), keys_words[0].bitcast(I32))
+        query_raw = sb.tile([P, PACK, Q], F32, name="query_raw", tag="slot_3", align_bytes=64)
+        nc.sync.dma_start(query_raw[:], query.rearrange("(p j) q -> p j q", j=PACK))
+
+        key_scales = sb.tile([P, T], U8, name="key_scales", align_bytes=64)
+        nc.gpsimd.memset(key_scales[:].bitcast(I32), 0)
+        for quad in range(P // QUADRANT):
+            nc.scalar.dma_start(
+                key_scales[QUADRANT * quad : QUADRANT * quad + 4, :].bitcast(I32),
+                keys_scales[0, 4 * quad : 4 * quad + 4, :].bitcast(I32),
+            )
+        os_col = sb.tile([P, PACK], F32, name="os_col")
+        nc.scalar.dma_start(os_col[:], slot_factor.rearrange("o (p t) -> p (o t)", t=PACK))
+        identity = sb.tile([P, P], F32, name="identity")
+        make_identity(nc, identity[:])
+
+        vals_planes = vals.rearrange("(p t) c -> p t c", t=PACK)
+
+        def load_vals(t):
+            plane = sb.tile([P, T], F32, name=f"vals{t}", tag=f"slot_{t}", align_bytes=64)
+            nc.sync.dma_start(plane[:], vals_planes[:, t, :])
+            return plane
+
+        ratio = sb.tile([P, HALVES], F32, name="ratio")
+        rest = sb.tile([P, HALVES], F32, name="rest", tag="slot_0", align_bytes=64)
+        rest_inv = sb.tile([P, HALVES], F32, name="rest_inv", tag="slot_1", align_bytes=64)
+        nc.vector.tensor_scalar(rest[:], share_col[:], 1.0, TINY, ALU.subtract, ALU.subtract)
+        nc.vector.reciprocal(rest_inv[:], rest[:])
+        nc.vector.tensor_scalar(ratio[:], rest_inv[:], -2.0 / 3.0, 1.0 / 3.0, ALU.mult, ALU.add)
+        planes = [load_vals(0), load_vals(1)]
+
+        got_scales = sb.tile([P, SLOTS], U8, name="got_scales", align_bytes=64)
+        got_words = sb.tile([P, SLOTS], U16, name="got_words", align_bytes=64)
+        nc.vector.tensor_copy(got_words[:], key_words[:].indirect(offsets[:]))
+        nc.vector.tensor_copy(got_scales[:], key_scales[:].indirect(offsets[:]))
+
+        scores = []
+        for h in range(HALVES):
+            q_bf = sb.tile([P, P, PACK], BF16, name=f"q_bf{h}", align_bytes=64)
+            nc.scalar.copy(
+                q_bf[:].rearrange("p (c i) j -> p c j i", i=4),
+                query_raw[:, :, h * P : (h + 1) * P].rearrange("p j (c i) -> p c j i", i=4),
+            )
+            q_codes = sb.tile([P, P], U32, name=f"q_codes{h}", align_bytes=64)
+            q_scales = sb.tile([P, P], U8, name=f"q_scales{h}", align_bytes=64)
+            nc.vector.quantize_mx(q_codes[:].bitcast(FP8X4), q_scales[:], q_bf[:].rearrange("p q j -> p (q j)"))
+            score = ps.tile([P, SLOTS], F32, name=f"score{h}")
+            nc.tensor.matmul_mx(
+                score[:],
+                lhsT=q_codes[:].bitcast(FP8X4),
+                lhsT_scale=q_scales[:],
+                rhs=got_words[:].bitcast(FP4X4),
+                rhs_scale=got_scales[:],
+                start=True,
+                stop=True,
+            )
+            scores.append(score)
+
+        planes.append(load_vals(2))
+        planes.append(load_vals(3))
+
+        os_rows = ps.tile([P, PACK, P], F32, name="os_rows")
+        for t in range(PACK):
+            nc.tensor.transpose(os_rows[:, t, :], os_col[:, t : t + 1].to_broadcast([P, P]), identity[:])
+
+        def turn_and_quantise(rows_bf, turned, name):
+            words = rows_bf[:].bitcast(F32)
+            for u in range(2):
+                nc.tensor.transpose(turned[:, u, :], words[:, u : SLOTS // 2 : 2], identity[:])
+            grouped = sb.tile([P, P, 2], F32, name=f"{name}_grouped", align_bytes=64)
+            nc.scalar.copy(grouped[:], turned.rearrange("s u c -> s c u"))
+            codes = sb.tile([P, P], U32, name=f"{name}_codes", align_bytes=64)
+            scales = sb.tile([P, P], U8, name=f"{name}_scales", align_bytes=64)
+            nc.vector.quantize_mx(
+                codes[:].bitcast(FP8X4), scales[:], grouped[:].rearrange("s c u -> s (c u)").bitcast(BF16)
+            )
+            return codes, scales
+
+        neg_max, tanhs, exps = [], [], []
+        for h in range(HALVES):
+            m = sb.tile([P, 1], F32, name=f"neg_max{h}")
+            nc.vector.tensor_reduce(m[:], scores[h][:], AXIS.X, ALU.max, negate=True)
+            neg_max.append(m)
+        for h in range(HALVES):
+            ex = sb.tile([P, SLOTS], F32, name=f"exp{h}")
+            nc.scalar.activation(ex[:], scores[h][:], ACT.Exp, bias=neg_max[h][:], scale=1.0)
+            th = sb.tile([P, SLOTS], F32, name=f"tanh{h}")
+            nc.scalar.activation(th[:], scores[h][:], ACT.Tanh, scale=0.5)
+            exps.append(ex)
+            tanhs.append(th)
+
+        def gather_vals(t):
+            got = sb.tile([P, SLOTS], BF16, name=f"got_vals{t}", align_bytes=64)
+            nc.vector.tensor_copy(got[:], planes[t][:].indirect(offsets[:]))
+            turned = ps.tile([P, 2, P], F32, name=f"v_turned{t}", tag=f"v_turned{t % 2}")
+            return turn_and_quantise(got, turned[:], f"v{t}")
+
+        v_ops = [gather_vals(0)]
+
+        w_turned = ps.tile([P, HALVES, 2, P], F32, name="w_turned")
+        w_ops = []
+        for h in range(HALVES):
+            part = sb.tile([P, SLOTS], F32, name=f"part{h}")
+            total = sb.tile([P, 1], F32, name=f"total{h}")
+            nc.vector.scalar_tensor_tensor(
+                part[:], tanhs[h][:], ratio[:, h : h + 1], exps[h][:], ALU.subtract, ALU.mult, accum_out=total[:]
+            )
+            total_inv = sb.tile([P, 1], F32, name=f"total_inv{h}")
+            nc.vector.reciprocal(total_inv[:], total[:])
+            w_bf = sb.tile([P, SLOTS], BF16, name=f"w_bf{h}", align_bytes=64)
+            nc.vector.scalar_tensor_tensor(
+                w_bf[:].rearrange("q (s t) -> q s t", t=PACK),
+                part[:].rearrange("q (s t) -> q s t", t=PACK),
+                total_inv[:],
+                os_rows[:].rearrange("q t s -> q s t"),
+                ALU.mult,
+                ALU.mult,
+            )
+            w_ops.append(turn_and_quantise(w_bf, w_turned[:, h], f"w{h}"))
+
+        result = [ps.tile([P, PACK, P], F32, name=f"result{h}") for h in range(HALVES)]
+        staged = sb.tile([P, PACK, Q], F32, name="staged")
+        out_planes = out_0.rearrange("(p t) q -> p t q", t=PACK)
+
+        def stage(t, h):
+            nc.scalar.copy(staged[:, t, h * P : (h + 1) * P], result[h][:, t, :])
+
+        for t in range(PACK):
+            if t > 0:
+                v_ops.append(gather_vals(t))
+            for h in range(HALVES):
+                nc.tensor.matmul_mx(
+                    result[h][:, t, :],
+                    lhsT=v_ops[t][0][:].bitcast(FP8X4),
+                    lhsT_scale=v_ops[t][1][:],
+                    rhs=w_ops[h][0][:].bitcast(FP8X4),
+                    rhs_scale=w_ops[h][1][:],
+                    start=True,
+                    stop=True,
+                )
+            if t < PACK - 1:
+                for h in range(HALVES):
+                    stage(t, h)
+        nc.sync.dma_start(out_planes[:, : PACK - 1, :], staged[:, : PACK - 1, :])
+
+        o_bf = [sb.tile([P, P, PACK], BF16, name=f"o_bf{h}", align_bytes=64) for h in range(HALVES)]
+        nc.vector.tensor_copy(o_bf[0][:], result[0][:].rearrange("p t q -> p q t"))
+        nc.scalar.copy(o_bf[1][:], result[1][:].rearrange("p t q -> p q t"))
+        for h in reversed(range(HALVES)):
+            stage(PACK - 1, h)
+        nc.sync.dma_start(out_planes[:, PACK - 1, :], staged[:, PACK - 1, :])
+
+        o_codes = sb.tile([P, Q], U32, name="o_codes", align_bytes=64)
+        o_scales = sb.tile([P, Q], U8, name="o_scales", align_bytes=64)
+        for h in reversed(range(HALVES)):
+            cols = slice(h * P, (h + 1) * P)
+            nc.vector.quantize_mx(
+                o_codes[:, cols].bitcast(FP8X4), o_scales[:, cols], o_bf[h][:].rearrange("p q t -> p (q t)")
+            )
+        nc.sync.dma_start(out_1[0].rearrange("p c r -> p (c r)").bitcast(I32), o_codes[:].bitcast(I32))
+        for quad in range(P // QUADRANT):
+            queue = nc.scalar if quad % 2 == 0 else nc.sync
+            queue.dma_start(
+                out_2[0, 4 * quad : 4 * quad + 4, :].bitcast(I32),
+                o_scales[QUADRANT * quad : QUADRANT * quad + 4, :].bitcast(I32),
+            )

@@ -23,6 +23,8 @@ PACK = 4
 HALVES = Q // P
 QUADRANT = 32
 TINY = 1e-30
+SCALAR_PLANE = 1
+CAST_COLS = 1024
 
 
 def tile_attend_mixedparts_pl_kernel(tc, query, keys_words, keys_scales, share, slot_factor, vals, offs, out_0, out_1, out_2):
@@ -34,45 +36,46 @@ def tile_attend_mixedparts_pl_kernel(tc, query, keys_words, keys_scales, share, 
         offsets = sb.tile([P, SLOTS // 16], U16, name="offsets")
         nc.sync.dma_start(offsets[:], offs)
 
-        share_col = sb.tile([P, HALVES], F32, name="share_col")
+        share_col = sb.tile([P, HALVES], F32, name="share_col", tag="slot_share", align_bytes=64)
         with nc.allow_non_contiguous_dma(reason="one share for each partition and half"):
             nc.sync.dma_start(share_col[:], share.rearrange("(h p) o -> p (h o)", p=P))
-        key_words = sb.tile([P, T], U16, name="key_words", tag="slot_2", align_bytes=64)
+        key_words = sb.tile([P, T], U16, name="key_words", tag="slot_words", align_bytes=64)
         nc.sync.dma_start(key_words[:].bitcast(I32), keys_words[0].bitcast(I32))
-        query_raw = sb.tile([P, PACK, Q], F32, name="query_raw", tag="slot_3", align_bytes=64)
+        query_raw = sb.tile([P, PACK, Q], F32, name="query_raw", tag="slot_query", align_bytes=64)
         nc.sync.dma_start(query_raw[:], query.rearrange("(p j) q -> p j q", j=PACK))
-
-        key_scales = sb.tile([P, T], U8, name="key_scales", align_bytes=64)
+        key_scales = sb.tile([P, T], U8, name="key_scales", tag="slot_scales", align_bytes=64)
         nc.gpsimd.memset(key_scales[:].bitcast(I32), 0)
         for quad in range(P // QUADRANT):
             nc.scalar.dma_start(
                 key_scales[QUADRANT * quad : QUADRANT * quad + 4, :].bitcast(I32),
                 keys_scales[0, 4 * quad : 4 * quad + 4, :].bitcast(I32),
             )
-        os_col = sb.tile([P, PACK], F32, name="os_col")
-        nc.scalar.dma_start(os_col[:], slot_factor.rearrange("o (p t) -> p (o t)", t=PACK))
         identity = sb.tile([P, P], F32, name="identity")
         make_identity(nc, identity[:])
 
         vals_planes = vals.rearrange("(p t) c -> p t c", t=PACK)
 
-        def load_vals(t):
-            plane = sb.tile([P, T], F32, name=f"vals{t}", tag=f"slot_{t}", align_bytes=64)
+        def load_vals(t, slot):
+            plane = sb.tile([P, T], F32, name=f"vals{t}", tag=slot, align_bytes=64)
             nc.sync.dma_start(plane[:], vals_planes[:, t, :])
             return plane
 
         ratio = sb.tile([P, HALVES], F32, name="ratio")
-        rest = sb.tile([P, HALVES], F32, name="rest", tag="slot_0", align_bytes=64)
-        rest_inv = sb.tile([P, HALVES], F32, name="rest_inv", tag="slot_1", align_bytes=64)
+        rest = sb.tile([P, HALVES], F32, name="rest", tag="slot_rest")
+        rest_inv = sb.tile([P, HALVES], F32, name="rest_inv")
         nc.vector.tensor_scalar(rest[:], share_col[:], 1.0, TINY, ALU.subtract, ALU.subtract)
+        planes = [load_vals(0, "slot_share")]
         nc.vector.reciprocal(rest_inv[:], rest[:])
         nc.vector.tensor_scalar(ratio[:], rest_inv[:], -2.0 / 3.0, 1.0 / 3.0, ALU.mult, ALU.add)
-        planes = [load_vals(0), load_vals(1)]
+        os_col = sb.tile([P, PACK], F32, name="os_col", tag="slot_rest")
+        nc.sync.dma_start(os_col[:], slot_factor.rearrange("o (p t) -> p (o t)", t=PACK))
 
         got_scales = sb.tile([P, SLOTS], U8, name="got_scales", align_bytes=64)
-        got_words = sb.tile([P, SLOTS], U16, name="got_words", align_bytes=64)
+        got_words = sb.tile([P, SLOTS], U16, name="got_words", tag="slot_got_words", align_bytes=64)
         nc.vector.tensor_copy(got_words[:], key_words[:].indirect(offsets[:]))
+        planes.append(load_vals(1, "slot_words"))
         nc.vector.tensor_copy(got_scales[:], key_scales[:].indirect(offsets[:]))
+        planes.append(load_vals(2, "slot_scales"))
 
         scores = []
         for h in range(HALVES):
@@ -84,7 +87,7 @@ def tile_attend_mixedparts_pl_kernel(tc, query, keys_words, keys_scales, share, 
             q_codes = sb.tile([P, P], U32, name=f"q_codes{h}", align_bytes=64)
             q_scales = sb.tile([P, P], U8, name=f"q_scales{h}", align_bytes=64)
             nc.vector.quantize_mx(q_codes[:].bitcast(FP8X4), q_scales[:], q_bf[:].rearrange("p q j -> p (q j)"))
-            score = ps.tile([P, SLOTS], F32, name=f"score{h}")
+            score = ps.tile([P, SLOTS], F32, name=f"score{h}", tag=f"bank_half{h}")
             nc.tensor.matmul_mx(
                 score[:],
                 lhsT=q_codes[:].bitcast(FP8X4),
@@ -96,99 +99,149 @@ def tile_attend_mixedparts_pl_kernel(tc, query, keys_words, keys_scales, share, 
             )
             scores.append(score)
 
-        planes.append(load_vals(2))
-        planes.append(load_vals(3))
+        planes.append(load_vals(3, "slot_query"))
 
-        os_rows = ps.tile([P, PACK, P], F32, name="os_rows")
+
+        os_rows = ps.tile([P, PACK, P], F32, name="os_rows", tag="bank_os")
         for t in range(PACK):
             nc.tensor.transpose(os_rows[:, t, :], os_col[:, t : t + 1].to_broadcast([P, P]), identity[:])
 
-        def turn_and_quantise(rows_bf, turned, name):
+        def turn(rows_bf, turned):
             words = rows_bf[:].bitcast(F32)
             for u in range(2):
                 nc.tensor.transpose(turned[:, u, :], words[:, u : SLOTS // 2 : 2], identity[:])
-            grouped = sb.tile([P, P, 2], F32, name=f"{name}_grouped", align_bytes=64)
-            nc.scalar.copy(grouped[:], turned.rearrange("s u c -> s c u"))
-            codes = sb.tile([P, P], U32, name=f"{name}_codes", align_bytes=64)
-            scales = sb.tile([P, P], U8, name=f"{name}_scales", align_bytes=64)
+
+        def quantise(grouped, name, codes):
+            scales = sb.tile([P, grouped.shape[1]], U8, name=f"{name}_scales", align_bytes=64)
             nc.vector.quantize_mx(
-                codes[:].bitcast(FP8X4), scales[:], grouped[:].rearrange("s c u -> s (c u)").bitcast(BF16)
+                codes.bitcast(FP8X4), scales[:], grouped[:].rearrange("s c u -> s (c u)").bitcast(BF16)
             )
             return codes, scales
 
         neg_max, tanhs, exps = [], [], []
         for h in range(HALVES):
-            m = sb.tile([P, 1], F32, name=f"neg_max{h}")
+            m = sb.tile([P, 1], F32, name=f"neg_max{h}", tag=f"slot_neg_max{h}", align_bytes=64)
             nc.vector.tensor_reduce(m[:], scores[h][:], AXIS.X, ALU.max, negate=True)
             neg_max.append(m)
         for h in range(HALVES):
-            ex = sb.tile([P, SLOTS], F32, name=f"exp{h}")
-            nc.scalar.activation(ex[:], scores[h][:], ACT.Exp, bias=neg_max[h][:], scale=1.0)
             th = sb.tile([P, SLOTS], F32, name=f"tanh{h}")
             nc.scalar.activation(th[:], scores[h][:], ACT.Tanh, scale=0.5)
-            exps.append(ex)
             tanhs.append(th)
+        for h in range(HALVES):
+            ex = sb.tile([P, SLOTS], F32, name=f"exp{h}")
+            nc.scalar.activation(ex[:], scores[h][:], ACT.Exp, bias=neg_max[h][:], scale=1.0)
+            exps.append(ex)
+
+        got_slots = ["slot_got_words", "slot_got1", "slot_part1", "slot_scales"]
+        turned_banks = ["bank_v0", "bank_v1", "bank_v2", "bank_half1"]
 
         def gather_vals(t):
-            got = sb.tile([P, SLOTS], BF16, name=f"got_vals{t}", align_bytes=64)
-            nc.vector.tensor_copy(got[:], planes[t][:].indirect(offsets[:]))
-            turned = ps.tile([P, 2, P], F32, name=f"v_turned{t}", tag=f"v_turned{t % 2}")
-            return turn_and_quantise(got, turned[:], f"v{t}")
+            got = sb.tile([P, SLOTS], BF16, name=f"got_vals{t}", tag=got_slots[t], align_bytes=64)
+            if t == SCALAR_PLANE:
+                rounded = sb.tile([P, T], BF16, name="vals_rounded", tag="slot_neg_max1", align_bytes=64)
+                for c in range(0, T, CAST_COLS):
+                    nc.scalar.activation(rounded[:, c : c + CAST_COLS], planes[t][:, c : c + CAST_COLS], ACT.Copy)
+                nc.scalar.activation(got[:], rounded[:].indirect(offsets[:]), ACT.Copy)
+            else:
+                nc.vector.tensor_copy(got[:], planes[t][:].indirect(offsets[:]))
+            return got
 
-        v_ops = [gather_vals(0)]
+        def group_vals(t):
+            turned = ps.tile([P, 2, P], F32, name=f"v_turned{t}", tag=turned_banks[t])
+            turn(got_vals[t], turned)
+            grouped = sb.tile([P, P, 2], F32, name=f"v_grouped{t}", tag=f"slot_v_grouped{t}", align_bytes=64)
+            nc.scalar.copy(grouped[:], turned[:].rearrange("s u c -> s c u"))
+            return grouped
 
-        w_turned = ps.tile([P, HALVES, 2, P], F32, name="w_turned")
-        w_ops = []
+        got_vals = [gather_vals(0)]
+        first_codes = sb.tile([P, P], U32, name="first_codes", align_bytes=64)
+        v_ops = [quantise(group_vals(0), "v0", first_codes[:])]
+        got_vals.append(gather_vals(1))
+
+        parts, totals, total_invs = [], [], []
         for h in range(HALVES):
-            part = sb.tile([P, SLOTS], F32, name=f"part{h}")
+            part = sb.tile([P, SLOTS], F32, name=f"part{h}", tag=f"slot_part{h}", align_bytes=64)
             total = sb.tile([P, 1], F32, name=f"total{h}")
             nc.vector.scalar_tensor_tensor(
-                part[:], tanhs[h][:], ratio[:, h : h + 1], exps[h][:], ALU.subtract, ALU.mult, accum_out=total[:]
+                part[:], tanhs[h][:], ratio[:, h : h + 1], exps[h][:], ALU.subtract, ALU.mult,
+                accum_out=total[:],
             )
+            parts.append(part)
+            totals.append(total)
+        for h in range(HALVES):
             total_inv = sb.tile([P, 1], F32, name=f"total_inv{h}")
-            nc.vector.reciprocal(total_inv[:], total[:])
+            nc.vector.reciprocal(total_inv[:], totals[h][:])
+            total_invs.append(total_inv)
+        w_turned = ps.tile([P, HALVES, 2, P], F32, name="w_turned", tag="bank_half0")
+        for h in range(HALVES):
             w_bf = sb.tile([P, SLOTS], BF16, name=f"w_bf{h}", align_bytes=64)
             nc.vector.scalar_tensor_tensor(
                 w_bf[:].rearrange("q (s t) -> q s t", t=PACK),
-                part[:].rearrange("q (s t) -> q s t", t=PACK),
-                total_inv[:],
+                parts[h][:].rearrange("q (s t) -> q s t", t=PACK),
+                total_invs[h][:],
                 os_rows[:].rearrange("q t s -> q s t"),
                 ALU.mult,
                 ALU.mult,
             )
-            w_ops.append(turn_and_quantise(w_bf, w_turned[:, h], f"w{h}"))
+            turn(w_bf, w_turned[:, h])
+        w_grouped = sb.tile([P, Q, 2], F32, name="w_grouped", tag="slot_neg_max1", align_bytes=64)
+        nc.scalar.copy(
+            w_grouped[:].rearrange("s (h c) u -> s h c u", h=HALVES), w_turned[:].rearrange("s h u c -> s h c u")
+        )
 
-        result = [ps.tile([P, PACK, P], F32, name=f"result{h}") for h in range(HALVES)]
+        got_vals.append(gather_vals(2))
+        got_vals.append(gather_vals(3))
+        late_codes = sb.tile([P, Q + (PACK - 1) * P], U32, name="late_codes", tag="slot_query", align_bytes=64)
+        w_codes, w_scales = quantise(w_grouped, "w", late_codes[:, :Q])
+        for t in range(1, PACK):
+            v_ops.append(quantise(group_vals(t), f"v{t}", late_codes[:, Q + (t - 1) * P : Q + t * P]))
+
+        result_banks = [["bank_os", "bank_v0"], ["bank_late0", "bank_late1"]]
         staged = sb.tile([P, PACK, Q], F32, name="staged")
         out_planes = out_0.rearrange("(p t) q -> p t q", t=PACK)
-
-        def stage(t, h):
-            nc.scalar.copy(staged[:, t, h * P : (h + 1) * P], result[h][:, t, :])
-
-        for t in range(PACK):
-            if t > 0:
-                v_ops.append(gather_vals(t))
-            for h in range(HALVES):
-                nc.tensor.matmul_mx(
-                    result[h][:, t, :],
-                    lhsT=v_ops[t][0][:].bitcast(FP8X4),
-                    lhsT_scale=v_ops[t][1][:],
-                    rhs=w_ops[h][0][:].bitcast(FP8X4),
-                    rhs_scale=w_ops[h][1][:],
-                    start=True,
-                    stop=True,
-                )
-            if t < PACK - 1:
-                for h in range(HALVES):
-                    stage(t, h)
-        nc.sync.dma_start(out_planes[:, : PACK - 1, :], staged[:, : PACK - 1, :])
-
         o_bf = [sb.tile([P, P, PACK], BF16, name=f"o_bf{h}", align_bytes=64) for h in range(HALVES)]
-        nc.vector.tensor_copy(o_bf[0][:], result[0][:].rearrange("p t q -> p q t"))
-        nc.scalar.copy(o_bf[1][:], result[1][:].rearrange("p t q -> p q t"))
-        for h in reversed(range(HALVES)):
-            stage(PACK - 1, h)
-        nc.sync.dma_start(out_planes[:, PACK - 1, :], staged[:, PACK - 1, :])
+
+        def multiply(pair):
+            banks = [
+                ps.tile([P, 2, P], F32, name=f"result{pair}_{h}", tag=result_banks[pair][h]) for h in range(HALVES)
+            ]
+            for k in range(2):
+                codes, scales = v_ops[2 * pair + k]
+                for h in range(HALVES):
+                    cols = slice(h * P, (h + 1) * P)
+                    nc.tensor.matmul_mx(
+                        banks[h][:, k, :],
+                        lhsT=codes.bitcast(FP8X4),
+                        lhsT_scale=scales[:],
+                        rhs=w_codes[:, cols].bitcast(FP8X4),
+                        rhs_scale=w_scales[:, cols],
+                        start=True,
+                        stop=True,
+                    )
+            return banks
+
+        def stage(pair, h, bank):
+            nc.scalar.copy(staged[:, 2 * pair : 2 * pair + 2, h * P : (h + 1) * P], bank[:])
+
+        def round_pair(copy, pair, h, bank):
+            copy(o_bf[h][:, :, 2 * pair : 2 * pair + 2], bank[:].rearrange("p k q -> p q k"))
+
+        def store(pair):
+            nc.sync.dma_start(out_planes[:, 2 * pair : 2 * pair + 2, :], staged[:, 2 * pair : 2 * pair + 2, :])
+
+        banks = multiply(0)
+        round_pair(nc.vector.tensor_copy, 0, 0, banks[0])
+        stage(0, 1, banks[1])
+        round_pair(nc.vector.tensor_copy, 0, 1, banks[1])
+        stage(0, 0, banks[0])
+        store(0)
+
+        banks = multiply(1)
+        round_pair(nc.vector.tensor_copy, 1, 0, banks[0])
+        round_pair(nc.scalar.copy, 1, 1, banks[1])
+        stage(1, 1, banks[1])
+        stage(1, 0, banks[0])
+        store(1)
 
         o_codes = sb.tile([P, Q], U32, name="o_codes", align_bytes=64)
         o_scales = sb.tile([P, Q], U8, name="o_scales", align_bytes=64)

from contextlib import ExitStack

import concourse.mybir as mybir
from concourse.masks import make_identity

D, E, T, SLOTS, Q = 512, 512, 2048, 512, 256
FLOPS = 2 * Q * SLOTS * D + 2 * E * SLOTS * Q

F32 = mybir.dt.float32
BF16 = mybir.dt.bfloat16
I32 = mybir.dt.int32
U32 = mybir.dt.uint32
U16 = mybir.dt.uint16
U8 = mybir.dt.uint8
FP8X4 = mybir.dt.float8_e4m3fn_x4
FP4X4 = mybir.dt.float4_e2m1fn_x4
ALU = mybir.AluOpType
ACT = mybir.ActivationFunctionType
AXIS = mybir.AxisListType

P = 128
PACK = 4
HALVES = Q // P
QUADRANT = 32
TINY = 1e-30
SCALAR_PLANE = 1
CAST_COLS = 1024


def tile_attend_mixedparts_pl_kernel(tc, query, keys_words, keys_scales, share, slot_factor, vals, offs, out_0, out_1, out_2):
    nc = tc.nc
    with ExitStack() as ctx:
        sb = ctx.enter_context(tc.tile_pool(name="sb", bufs=1))
        ps = ctx.enter_context(tc.psum_pool(name="ps", bufs=1))

        offsets = sb.tile([P, SLOTS // 16], U16, name="offsets")
        nc.sync.dma_start(offsets[:], offs)

        share_col = sb.tile([P, HALVES], F32, name="share_col", tag="slot_share", align_bytes=64)
        with nc.allow_non_contiguous_dma(reason="one share for each partition and half"):
            nc.sync.dma_start(share_col[:], share.rearrange("(h p) o -> p (h o)", p=P))
        key_words = sb.tile([P, T], U16, name="key_words", tag="slot_words", align_bytes=64)
        nc.sync.dma_start(key_words[:].bitcast(I32), keys_words[0].bitcast(I32))
        query_raw = sb.tile([P, PACK, Q], F32, name="query_raw", tag="slot_query", align_bytes=64)
        nc.sync.dma_start(query_raw[:], query.rearrange("(p j) q -> p j q", j=PACK))
        key_scales = sb.tile([P, T], U8, name="key_scales", tag="slot_scales", align_bytes=64)
        nc.gpsimd.memset(key_scales[:].bitcast(I32), 0)
        for quad in range(P // QUADRANT):
            nc.scalar.dma_start(
                key_scales[QUADRANT * quad : QUADRANT * quad + 4, :].bitcast(I32),
                keys_scales[0, 4 * quad : 4 * quad + 4, :].bitcast(I32),
            )
        identity = sb.tile([P, P], F32, name="identity")
        make_identity(nc, identity[:])

        vals_planes = vals.rearrange("(p t) c -> p t c", t=PACK)

        def load_vals(t, slot):
            plane = sb.tile([P, T], F32, name=f"vals{t}", tag=slot, align_bytes=64)
            nc.sync.dma_start(plane[:], vals_planes[:, t, :])
            return plane

        ratio = sb.tile([P, HALVES], F32, name="ratio")
        rest = sb.tile([P, HALVES], F32, name="rest", tag="slot_rest")
        rest_inv = sb.tile([P, HALVES], F32, name="rest_inv")
        nc.vector.tensor_scalar(rest[:], share_col[:], 1.0, TINY, ALU.subtract, ALU.subtract)
        planes = [load_vals(0, "slot_share")]
        nc.vector.reciprocal(rest_inv[:], rest[:])
        nc.vector.tensor_scalar(ratio[:], rest_inv[:], -2.0 / 3.0, 1.0 / 3.0, ALU.mult, ALU.add)
        os_col = sb.tile([P, PACK], F32, name="os_col", tag="slot_rest")
        nc.sync.dma_start(os_col[:], slot_factor.rearrange("o (p t) -> p (o t)", t=PACK))

        got_scales = sb.tile([P, SLOTS], U8, name="got_scales", align_bytes=64)
        got_words = sb.tile([P, SLOTS], U16, name="got_words", tag="slot_got_words", align_bytes=64)
        nc.vector.tensor_copy(got_words[:], key_words[:].indirect(offsets[:]))
        planes.append(load_vals(1, "slot_words"))
        nc.vector.tensor_copy(got_scales[:], key_scales[:].indirect(offsets[:]))
        planes.append(load_vals(2, "slot_scales"))

        scores = []
        for h in range(HALVES):
            q_bf = sb.tile([P, P, PACK], BF16, name=f"q_bf{h}", align_bytes=64)
            nc.scalar.copy(
                q_bf[:].rearrange("p (c i) j -> p c j i", i=4),
                query_raw[:, :, h * P : (h + 1) * P].rearrange("p j (c i) -> p c j i", i=4),
            )
            q_codes = sb.tile([P, P], U32, name=f"q_codes{h}", align_bytes=64)
            q_scales = sb.tile([P, P], U8, name=f"q_scales{h}", align_bytes=64)
            nc.vector.quantize_mx(q_codes[:].bitcast(FP8X4), q_scales[:], q_bf[:].rearrange("p q j -> p (q j)"))
            score = ps.tile([P, SLOTS], F32, name=f"score{h}", tag=f"bank_half{h}")
            nc.tensor.matmul_mx(
                score[:],
                lhsT=q_codes[:].bitcast(FP8X4),
                lhsT_scale=q_scales[:],
                rhs=got_words[:].bitcast(FP4X4),
                rhs_scale=got_scales[:],
                start=True,
                stop=True,
            )
            scores.append(score)

        planes.append(load_vals(3, "slot_query"))


        os_rows = ps.tile([P, PACK, P], F32, name="os_rows", tag="bank_os")
        for t in range(PACK):
            nc.tensor.transpose(os_rows[:, t, :], os_col[:, t : t + 1].to_broadcast([P, P]), identity[:])

        def turn(rows_bf, turned):
            words = rows_bf[:].bitcast(F32)
            for u in range(2):
                nc.tensor.transpose(turned[:, u, :], words[:, u : SLOTS // 2 : 2], identity[:])

        def quantise(grouped, name, codes):
            scales = sb.tile([P, grouped.shape[1]], U8, name=f"{name}_scales", align_bytes=64)
            nc.vector.quantize_mx(
                codes.bitcast(FP8X4), scales[:], grouped[:].rearrange("s c u -> s (c u)").bitcast(BF16)
            )
            return codes, scales

        neg_max, tanhs, exps = [], [], []
        for h in range(HALVES):
            m = sb.tile([P, 1], F32, name=f"neg_max{h}", tag=f"slot_neg_max{h}", align_bytes=64)
            nc.vector.tensor_reduce(m[:], scores[h][:], AXIS.X, ALU.max, negate=True)
            neg_max.append(m)
        for h in range(HALVES):
            th = sb.tile([P, SLOTS], F32, name=f"tanh{h}")
            nc.scalar.activation(th[:], scores[h][:], ACT.Tanh, scale=0.5)
            tanhs.append(th)
        for h in range(HALVES):
            ex = sb.tile([P, SLOTS], F32, name=f"exp{h}")
            nc.scalar.activation(ex[:], scores[h][:], ACT.Exp, bias=neg_max[h][:], scale=1.0)
            exps.append(ex)

        got_slots = ["slot_got_words", "slot_got1", "slot_part1", "slot_scales"]
        turned_banks = ["bank_v0", "bank_v1", "bank_v2", "bank_half1"]

        def gather_vals(t):
            got = sb.tile([P, SLOTS], BF16, name=f"got_vals{t}", tag=got_slots[t], align_bytes=64)
            if t == SCALAR_PLANE:
                rounded = sb.tile([P, T], BF16, name="vals_rounded", tag="slot_neg_max1", align_bytes=64)
                for c in range(0, T, CAST_COLS):
                    nc.scalar.activation(rounded[:, c : c + CAST_COLS], planes[t][:, c : c + CAST_COLS], ACT.Copy)
                nc.scalar.activation(got[:], rounded[:].indirect(offsets[:]), ACT.Copy)
            else:
                nc.vector.tensor_copy(got[:], planes[t][:].indirect(offsets[:]))
            return got

        def group_vals(t):
            turned = ps.tile([P, 2, P], F32, name=f"v_turned{t}", tag=turned_banks[t])
            turn(got_vals[t], turned)
            grouped = sb.tile([P, P, 2], F32, name=f"v_grouped{t}", tag=f"slot_v_grouped{t}", align_bytes=64)
            nc.scalar.copy(grouped[:], turned[:].rearrange("s u c -> s c u"))
            return grouped

        got_vals = [gather_vals(0)]
        first_codes = sb.tile([P, P], U32, name="first_codes", align_bytes=64)
        v_ops = [quantise(group_vals(0), "v0", first_codes[:])]
        got_vals.append(gather_vals(1))

        parts, totals, total_invs = [], [], []
        for h in range(HALVES):
            part = sb.tile([P, SLOTS], F32, name=f"part{h}", tag=f"slot_part{h}", align_bytes=64)
            total = sb.tile([P, 1], F32, name=f"total{h}")
            nc.vector.scalar_tensor_tensor(
                part[:], tanhs[h][:], ratio[:, h : h + 1], exps[h][:], ALU.subtract, ALU.mult,
                accum_out=total[:],
            )
            parts.append(part)
            totals.append(total)
        for h in range(HALVES):
            total_inv = sb.tile([P, 1], F32, name=f"total_inv{h}")
            nc.vector.reciprocal(total_inv[:], totals[h][:])
            total_invs.append(total_inv)
        w_turned = ps.tile([P, HALVES, 2, P], F32, name="w_turned", tag="bank_half0")
        for h in range(HALVES):
            w_bf = sb.tile([P, SLOTS], BF16, name=f"w_bf{h}", align_bytes=64)
            nc.vector.scalar_tensor_tensor(
                w_bf[:].rearrange("q (s t) -> q s t", t=PACK),
                parts[h][:].rearrange("q (s t) -> q s t", t=PACK),
                total_invs[h][:],
                os_rows[:].rearrange("q t s -> q s t"),
                ALU.mult,
                ALU.mult,
            )
            turn(w_bf, w_turned[:, h])
        w_grouped = sb.tile([P, Q, 2], F32, name="w_grouped", tag="slot_neg_max1", align_bytes=64)
        nc.scalar.copy(
            w_grouped[:].rearrange("s (h c) u -> s h c u", h=HALVES), w_turned[:].rearrange("s h u c -> s h c u")
        )

        got_vals.append(gather_vals(2))
        got_vals.append(gather_vals(3))
        late_codes = sb.tile([P, Q + (PACK - 1) * P], U32, name="late_codes", tag="slot_query", align_bytes=64)
        w_codes, w_scales = quantise(w_grouped, "w", late_codes[:, :Q])
        for t in range(1, PACK):
            v_ops.append(quantise(group_vals(t), f"v{t}", late_codes[:, Q + (t - 1) * P : Q + t * P]))

        result_banks = [["bank_os", "bank_v0"], ["bank_late0", "bank_late1"]]
        staged = sb.tile([P, PACK, Q], F32, name="staged")
        out_planes = out_0.rearrange("(p t) q -> p t q", t=PACK)
        o_bf = [sb.tile([P, P, PACK], BF16, name=f"o_bf{h}", align_bytes=64) for h in range(HALVES)]

        def multiply(pair):
            banks = [
                ps.tile([P, 2, P], F32, name=f"result{pair}_{h}", tag=result_banks[pair][h]) for h in range(HALVES)
            ]
            for k in range(2):
                codes, scales = v_ops[2 * pair + k]
                for h in range(HALVES):
                    cols = slice(h * P, (h + 1) * P)
                    nc.tensor.matmul_mx(
                        banks[h][:, k, :],
                        lhsT=codes.bitcast(FP8X4),
                        lhsT_scale=scales[:],
                        rhs=w_codes[:, cols].bitcast(FP8X4),
                        rhs_scale=w_scales[:, cols],
                        start=True,
                        stop=True,
                    )
            return banks

        def stage(pair, h, bank):
            nc.scalar.copy(staged[:, 2 * pair : 2 * pair + 2, h * P : (h + 1) * P], bank[:])

        def round_pair(copy, pair, h, bank):
            copy(o_bf[h][:, :, 2 * pair : 2 * pair + 2], bank[:].rearrange("p k q -> p q k"))

        def store(pair):
            nc.sync.dma_start(out_planes[:, 2 * pair : 2 * pair + 2, :], staged[:, 2 * pair : 2 * pair + 2, :])

        banks = multiply(0)
        round_pair(nc.vector.tensor_copy, 0, 0, banks[0])
        stage(0, 1, banks[1])
        round_pair(nc.vector.tensor_copy, 0, 1, banks[1])
        stage(0, 0, banks[0])
        store(0)

        banks = multiply(1)
        round_pair(nc.vector.tensor_copy, 1, 0, banks[0])
        round_pair(nc.scalar.copy, 1, 1, banks[1])
        stage(1, 1, banks[1])
        stage(1, 0, banks[0])
        store(1)

        o_codes = sb.tile([P, Q], U32, name="o_codes", align_bytes=64)
        o_scales = sb.tile([P, Q], U8, name="o_scales", align_bytes=64)
        for h in reversed(range(HALVES)):
            cols = slice(h * P, (h + 1) * P)
            nc.vector.quantize_mx(
                o_codes[:, cols].bitcast(FP8X4), o_scales[:, cols], o_bf[h][:].rearrange("p q t -> p (q t)")
            )
        nc.sync.dma_start(out_1[0].rearrange("p c r -> p (c r)").bitcast(I32), o_codes[:].bitcast(I32))
        for quad in range(P // QUADRANT):
            queue = nc.scalar if quad % 2 == 0 else nc.sync
            queue.dma_start(
                out_2[0, 4 * quad : 4 * quad + 4, :].bitcast(I32),
                o_scales[QUADRANT * quad : QUADRANT * quad + 4, :].bitcast(I32),
            )
